import numpy as np
import ml_dtypes


def mxq(x, axis, fmt="e4m3"):
    dtype, down = {"e4m3": (ml_dtypes.float8_e4m3fn, 7), "e5m2": (ml_dtypes.float8_e5m2, 14)}[fmt]
    v = np.moveaxis(np.asarray(x, np.float32).astype(ml_dtypes.bfloat16).astype(np.float64), axis, -1)
    blocks = v.reshape(v.shape[:-1] + (-1, 32))
    amax = np.abs(blocks).max(-1, keepdims=True)
    byte = np.maximum(np.where(amax > 0, np.frexp(amax)[1] - 1 + 127, 0) - down, 1)
    scale = np.exp2(byte - 127.0)
    codes = (blocks / scale).astype(np.float32).astype(dtype).astype(np.float64)
    return np.moveaxis((codes * scale).reshape(v.shape), -1, axis)


WIDE = False


def mx_kscale(k):
    if not WIDE:
        return np.ones(k)
    levels = np.array([30, -30])
    if k % 512:
        return np.exp2(np.random.permutation(np.resize(levels, k // 32))).repeat(32)
    a = np.empty((k // 512, 16))
    for p in range(k // 512):
        a[p, :8] = np.random.permutation(np.resize(levels, 8))
        for g in range(8):
            far = levels[np.abs(levels - a[p, g]) >= 10]
            a[p, g + 8] = far[np.random.randint(len(far))]
    return np.exp2(a.ravel()).repeat(32)


def f64(x):
    return np.asarray(x).astype(np.float64)


def striped(idx):
    return np.tile(np.asarray(idx).reshape(-1, 16).T, (8, 1)).astype(np.uint16)


def unstriped(offs):
    return offs[:16].T.reshape(-1).astype(np.int64)


E2M1 = np.array([0.0, 0.5, 1.0, 1.5, 2.0, 3.0, 4.0, 6.0, -0.0, -0.5, -1.0, -1.5, -2.0, -3.0, -4.0, -6.0])


def pack_weight(w, fmt):
    k, n = w.shape
    w = f64(np.asarray(w, np.float32).astype(ml_dtypes.bfloat16)).reshape(k // 32, 32, n)
    amax = np.abs(w).max(1)
    if fmt in ("e4m3", "e5m2"):
        byte = np.frexp(amax)[1] - 1 + 127 - (7 if fmt == "e4m3" else 14)
    else:
        mant, ex = np.frexp(amax / 6.0)
        byte = np.where(mant > 0.5, ex, ex - 1) + 127
    byte = np.clip(np.where(amax > 0, byte, 1), 1, 254)
    scaled = (w * np.exp2(127.0 - byte)[:, None, :]).reshape(k, n).astype(np.float32)
    by_word = np.ascontiguousarray(scaled.reshape(k // 512, 128, 4, n).transpose(0, 1, 3, 2))
    if fmt in ("e4m3", "e5m2"):
        words = by_word.astype(ml_dtypes.float8_e4m3fn if fmt == "e4m3" else ml_dtypes.float8_e5m2).view(np.uint8)
    else:
        c = by_word.astype(ml_dtypes.float4_e2m1fn).view(np.uint8) & 0xF
        words = (c[..., 0::2] | (c[..., 1::2] << 4)).reshape(k // 512, 128, 2 * n)
    return np.ascontiguousarray(words), np.ascontiguousarray(byte.astype(np.uint8).reshape(k // 512, 16, n))


def unpack_weight(words, scales, fmt):
    g, _, n = scales.shape
    words = np.ascontiguousarray(words).reshape(g, 128, n, -1)
    if fmt in ("e4m3", "e5m2"):
        vals = words.view(ml_dtypes.float8_e4m3fn if fmt == "e4m3" else ml_dtypes.float8_e5m2).astype(np.float64)
    else:
        nib = np.empty((g, 128, n, 4), np.uint8)
        nib[..., 0::2] = words & 0xF
        nib[..., 1::2] = words >> 4
        vals = E2M1[nib]
    vals = vals * np.repeat(np.exp2(scales.astype(np.float64) - 127.0), 8, axis=1)[..., None]
    return vals.transpose(0, 1, 3, 2).reshape(g * 512, n)


def sigmoid(v):
    return 1.0 / (1.0 + np.exp(-v))


def sgn(shape):
    return np.random.uniform(0.5, 2.0, shape) * np.where(np.random.standard_normal(shape) < 0, -1.0, 1.0)


K, T, J, R, F, Z, O, N = 512, 1024, 256, 512, 512, 1024, 128, 256


def setup_inputs():
    n = np.random.standard_normal
    idx = np.random.permutation(T)[:J]
    idx2 = np.random.permutation(Z)[:J]
    idx3 = np.random.permutation(J)[:O]
    idx4 = np.random.permutation(J)[:O]
    idx5 = np.random.permutation(J)[:O]
    idx6 = np.random.permutation(J)[:O]
    idx7 = np.random.permutation(T)[:O]
    fk = mx_kscale(K)
    ff = mx_kscale(F)
    fr = mx_kscale(R)
    xtp = pack_weight(n((K, T)) / fk[:, None], "e2m1")
    xop = pack_weight(n((F, Z)) / ff[:, None], "e5m2")
    wp = pack_weight(n((K, R)) * 1 / np.sqrt(K) * fk[:, None], "e5m2")
    w2p = pack_weight(n((F, R)) * 1 / np.sqrt(F) * ff[:, None], "e4m3")
    wbp = pack_weight(n((R, N)) * 1 / np.sqrt(R) / fr[:, None], "e4m3")
    wsp = pack_weight(n((K, N)) * 1 / np.sqrt(K) * fk[:, None], "e4m3")
    return {
        "xt_words": xtp[0],
        "xt_scales": xtp[1],
        "xo_words": xop[0],
        "xo_scales": xop[1],
        "w_words": wp[0],
        "w_scales": wp[1],
        "w2_words": w2p[0],
        "w2_scales": w2p[1],
        "sa": (np.random.uniform(0.5, 1.6, (R, 1)) * fr[:, None]).astype(np.float32),
        "sb": (np.random.uniform(0.5, 1.6, (R, 1)) * fr[:, None]).astype(np.float32),
        "sg": (sgn((R, 1))).astype(np.float32),
        "bg": (np.random.uniform(-2.0, 2.0, (R, 1))).astype(np.float32),
        "sh": (sgn((R, 1))).astype(np.float32),
        "bh": (np.random.uniform(-2.0, 2.0, (R, 1))).astype(np.float32),
        "wb_words": wbp[0],
        "wb_scales": wbp[1],
        "ws_words": wsp[0],
        "ws_scales": wsp[1],
        "offs": striped(idx),
        "offs2": striped(idx2),
        "offs3": striped(idx3),
        "offs4": striped(idx4),
        "offs5": striped(idx5),
        "offs6": striped(idx6),
        "offs7": striped(idx7),
    }


def reference(xt_words, xt_scales, xo_words, xo_scales, w_words, w_scales, w2_words, w2_scales, sa, sb, sg, bg, sh, bh, wb_words, wb_scales, ws_words, ws_scales, offs, offs2, offs3, offs4, offs5, offs6, offs7):
    idx = unstriped(offs)
    idx2 = unstriped(offs2)
    idx3 = unstriped(offs3)
    idx4 = unstriped(offs4)
    idx5 = unstriped(offs5)
    idx6 = unstriped(offs6)
    idx7 = unstriped(offs7)
    xtu = unpack_weight(xt_words, xt_scales, "e2m1")
    xou = unpack_weight(xo_words, xo_scales, "e5m2")
    wu = unpack_weight(w_words, w_scales, "e5m2")
    w2u = unpack_weight(w2_words, w2_scales, "e4m3")
    wbu = unpack_weight(wb_words, wb_scales, "e4m3")
    wsu = unpack_weight(ws_words, ws_scales, "e4m3")
    xtidxg = xtu[:, idx]
    a = wu.T @ xtidxg
    xoidx2g = xou[:, idx2]
    b = w2u.T @ xoidx2g
    u1 = a[:, idx3] * f64(sa) * sigmoid(b[:, idx4] * f64(sg) + f64(bg))
    u2 = b[:, idx5] * f64(sb) * sigmoid(a[:, idx6] * f64(sh) + f64(bh))
    hid = np.abs(u1 - u2)
    hidq = mxq(hid, 0, "e5m2")
    xtidx7g = xtu[:, idx7]
    y = wbu.T @ hidq + wsu.T @ xtidx7g
    return y

@@ -1,0 +1,212 @@
+from contextlib import ExitStack
+
+import concourse.mybir as mybir
+
+K, T, J, R, F, Z, O, N = 512, 1024, 256, 512, 512, 1024, 128, 256
+FLOPS = 2 * K * R * J + 2 * F * R * J + 2 * R * N * O + 2 * K * N * O
+
+F32 = mybir.dt.float32
+BF16 = mybir.dt.bfloat16
+I32 = mybir.dt.int32
+U32 = mybir.dt.uint32
+U16 = mybir.dt.uint16
+U8 = mybir.dt.uint8
+E4M3 = mybir.dt.float8_e4m3fn_x4
+E5M2 = mybir.dt.float8_e5m2_x4
+E2M1 = mybir.dt.float4_e2m1fn_x4
+ACT = mybir.ActivationFunctionType
+ALU = mybir.AluOpType
+
+P = 128
+PACK = 4
+QUADS = 4
+QUAD = 32
+WARM = False
+ABS_SPLIT = 64
+
+
+def tile_list_gatedcross_twotab_further_plain_kernel(
+    tc, xt_words, xt_scales, xo_words, xo_scales, w_words, w_scales, w2_words, w2_scales,
+    sa, sb, sg, bg, sh, bh, wb_words, wb_scales, ws_words, ws_scales,
+    offs, offs2, offs3, offs4, offs5, offs6, offs7, out,
+):
+    nc = tc.nc
+    with ExitStack() as ctx:
+        lists = ctx.enter_context(tc.tile_pool(name="lists", bufs=1))
+        sb_pool = ctx.enter_context(tc.tile_pool(name="sbuf", bufs=1))
+        psum = ctx.enter_context(tc.psum_pool(name="psum", bufs=1))
+
+        def new(name, shape, dtype):
+            return sb_pool.tile(shape, dtype, name=name, align_bytes=64)
+
+        def load_list(name, src):
+            tile = lists.tile(list(src.shape), U16, name=name)
+            nc.sync.dma_start(tile[:], src)
+            return tile
+
+        def load_words(name, src, dtype, queue):
+            flat = src[0] if len(src.shape) == 3 else src[0].rearrange("p n t -> p (n t)")
+            words = flat.bitcast(I32)
+            width = words.shape[1] * (2 if dtype == U16 else 1)
+            tile = new(name, [P, width], dtype)
+            queue.dma_start(tile[:].bitcast(I32), words)
+            return tile
+
+        def zeroed_rows(name, width):
+            tile = new(name, [P, width], U8)
+            nc.vector.memset(tile[:].bitcast(I32), 0)
+            return tile
+
+        def load_scales_direct(rows, src, queue):
+            words = src[0].bitcast(I32)
+            for q in range(QUADS):
+                queue.dma_start(rows[QUAD * q : QUAD * q + 4, :].bitcast(I32), words[4 * q : 4 * q + 4, :])
+
+        def load_scales_staged(name, src, queue):
+            words = src[0].bitcast(I32)
+            stage = new(name, [4, QUADS, words.shape[1]], I32)
+            queue.dma_start(stage[:], words.rearrange("(q r) n -> r q n", r=4))
+            return stage
+
+        def spread(rows, stage):
+            for q in range(QUADS):
+                nc.vector.tensor_copy(rows[QUAD * q : QUAD * q + 4, :].bitcast(I32), stage[:, q, :])
+
+        def load_vector(name, src, queue):
+            tile = new(name, [P, PACK], F32)
+            queue.dma_start(tile[:], src.rearrange("(p t) one -> p (t one)", t=PACK))
+            return tile
+
+        def deal_words(name, words, engine_copy):
+            dealt = new(name, [P, R], U32)
+            engine_copy(dealt[:].rearrange("p (t m) -> p m t", t=PACK), words[:].rearrange("p (m t) -> p m t", t=PACK))
+            return dealt
+
+        def deal_bytes(name, rows):
+            dealt = new(name, [P, R], U8)
+            nc.vector.tensor_copy(dealt[:].rearrange("p (t m) -> p t m", t=PACK), rows[:].rearrange("p (m t) -> p t m", t=PACK))
+            return dealt
+
+        def gather(name, window, offsets, dtype):
+            picked = new(name, [P, 16 * offsets.shape[1]], dtype)
+            nc.vector.tensor_copy(picked[:], window[:].indirect(offsets[:]))
+            return picked
+
+        xt_rows = zeroed_rows("xt_rows", T)
+        if WARM:
+            warm = new("warm", [P, 2], F32)
+            nc.vector.memset(warm[:, 0:1], 0.0)
+        w_rows = zeroed_rows("w_rows", R)
+        xo_rows = zeroed_rows("xo_rows", Z)
+        w2_rows = zeroed_rows("w2_rows", R)
+        ws_rows = new("ws_rows", [P, N], U8)
+        wb_rows = new("wb_rows", [P, N], U8)
+
+        l1 = load_list("l1", offs)
+        w_stage = load_scales_staged("w_stage", w_scales, nc.sync)
+        xt_w = load_words("xt_w", xt_words, U16, nc.sync)
+        w_w = load_words("w_w", w_words, U32, nc.sync)
+        load_scales_direct(xt_rows, xt_scales, nc.scalar)
+        if WARM:
+            nc.scalar.activation(warm[:, 1:2], warm[:, 0:1], ACT.Sigmoid)
+        sh_t = load_vector("sh_t", sh, nc.gpsimd)
+        bh_t = load_vector("bh_t", bh, nc.gpsimd)
+        sa_t = load_vector("sa_t", sa, nc.gpsimd)
+
+        l6 = load_list("l6", offs6)
+        l2 = load_list("l2", offs2)
+        xo_stage = load_scales_staged("xo_stage", xo_scales, nc.sync)
+        w2_stage = load_scales_staged("w2_stage", w2_scales, nc.sync)
+        xo_w = load_words("xo_w", xo_words, U32, nc.sync)
+        w2_w = load_words("w2_w", w2_words, U32, nc.sync)
+        l3 = load_list("l3", offs3)
+        l5 = load_list("l5", offs5)
+        sb_t = load_vector("sb_t", sb, nc.sync)
+        l4 = load_list("l4", offs4)
+        sg_t = load_vector("sg_t", sg, nc.sync)
+        bg_t = load_vector("bg_t", bg, nc.sync)
+        l7 = load_list("l7", offs7)
+        ws_w = load_words("ws_w", ws_words, U32, nc.sync)
+        load_scales_direct(ws_rows, ws_scales, nc.sync)
+        wb_w = load_words("wb_w", wb_words, U32, nc.sync)
+        load_scales_direct(wb_rows, wb_scales, nc.sync)
+
+        spread(w_rows, w_stage)
+        xt_gs = gather("xt_gs", xt_rows, l1, U8)
+        w_ds = deal_bytes("w_ds", w_rows)
+        xt_g = gather("xt_g", xt_w, l1, U16)
+        w_d = deal_words("w_d", w_w, nc.scalar.copy)
+
+        def product(tag, t, wd, wds, wfmt, xg, xgs, xfmt):
+            acc = psum.tile([P, J], F32, name=tag + str(t))
+            cols = slice(P * t, P * (t + 1))
+            nc.tensor.matmul_mx(acc[:], lhsT=wd[:, cols].bitcast(wfmt), lhsT_scale=wds[:, cols],
+                                rhs=xg[:].bitcast(xfmt), rhs_scale=xgs[:], start=True, stop=True)
+            return acc
+
+        a_ps = [product("bank_a", t, w_d, w_ds, E5M2, xt_g, xt_gs, E2M1) for t in range(PACK)]
+        a_sb = [new("a_sb" + str(t), [P, J], F32) for t in range(PACK)]
+        p1 = new("p1", [P, PACK, O], F32)
+        g2 = new("g2", [P, PACK, O], F32)
+        p2 = new("p2", [P, PACK, O], F32)
+        g1 = new("g1", [P, PACK, O], F32)
+
+        def look_a(t):
+            nc.scalar.activation(g2[:, t, :], a_sb[t][:].indirect(l6[:]), ACT.Sigmoid, bias=bh_t[:, t : t + 1], scale=sh_t[:, t : t + 1])
+            nc.scalar.activation(p1[:, t, :], a_sb[t][:].indirect(l3[:]), ACT.Copy, scale=sa_t[:, t : t + 1])
+
+        nc.vector.tensor_copy(a_sb[0][:], a_ps[0][:])
+        look_a(0)
+        nc.scalar.copy(a_sb[1][:], a_ps[1][:])
+        look_a(1)
+        nc.scalar.copy(a_sb[2][:], a_ps[2][:])
+        look_a(2)
+        nc.scalar.copy(a_sb[3][:], a_ps[3][:])
+        look_a(3)
+
+        spread(w2_rows, w2_stage)
+        spread(xo_rows, xo_stage)
+        w2_ds = deal_bytes("w2_ds", w2_rows)
+        xo_gs = gather("xo_gs", xo_rows, l2, U8)
+        xo_g = gather("xo_g", xo_w, l2, U32)
+        w2_d = deal_words("w2_d", w2_w, nc.vector.tensor_copy)
+        b_ps = [product("bank_b", t, w2_d, w2_ds, E4M3, xo_g, xo_gs, E5M2) for t in range(PACK)]
+        b_sb = [new("b_sb" + str(t), [P, J], F32) for t in range(PACK)]
+
+        x7_gs = gather("x7_gs", xt_rows, l7, U8)
+        x7_g = gather("x7_g", xt_w, l7, U16)
+        y_ps = [psum.tile([P, O], F32, name="bank_a" + str(h)) for h in range(N // P)]
+        for h in range(N // P):
+            cols = slice(P * h, P * (h + 1))
+            nc.tensor.matmul_mx(y_ps[h][:], lhsT=ws_w[:, cols].bitcast(E4M3), lhsT_scale=ws_rows[:, cols],
+                                rhs=x7_g[:].bitcast(E2M1), rhs_scale=x7_gs[:], start=True, stop=False)
+
+        u1 = new("u1", [P, PACK, O], F32)
+        u2 = new("u2", [P, PACK, O], F32)
+        diff = new("diff", [P, PACK, O], F32)
+        for t in range(PACK):
+            nc.vector.tensor_copy(b_sb[t][:], b_ps[t][:])
+        for t in range(PACK):
+            nc.scalar.activation(p2[:, t, :], b_sb[t][:].indirect(l5[:]), ACT.Copy, scale=sb_t[:, t : t + 1])
+            nc.scalar.activation(g1[:, t, :], b_sb[t][:].indirect(l4[:]), ACT.Sigmoid, bias=bg_t[:, t : t + 1], scale=sg_t[:, t : t + 1])
+            nc.vector.tensor_tensor(u2[:, t, :], p2[:, t, :], g2[:, t, :], ALU.mult)
+            nc.vector.tensor_tensor(u1[:, t, :], p1[:, t, :], g1[:, t, :], ALU.mult)
+            nc.vector.tensor_tensor(diff[:, t, :], u1[:, t, :], u2[:, t, :], ALU.subtract)
+
+        hid = new("hid", [P, O, PACK], BF16)
+        woven = diff[:].rearrange("p t o -> p o t")
+        nc.scalar.activation(hid[:, :ABS_SPLIT, :], woven[:, :ABS_SPLIT, :], ACT.Abs)
+        nc.vector.scalar_tensor_tensor(hid[:, ABS_SPLIT:, :], woven[:, ABS_SPLIT:, :], -1.0, woven[:, ABS_SPLIT:, :], ALU.mult, ALU.max)
+        hid_w = new("hid_w", [P, O], U32)
+        hid_s = new("hid_s", [P, O], U8)
+        nc.vector.quantize_mx(out=hid_w[:].bitcast(E5M2), scales=hid_s[:], in_=hid[:].rearrange("p o t -> p (o t)"))
+
+        y_sb = [new("y_sb" + str(h), [P, O], F32) for h in range(N // P)]
+        for h in range(N // P):
+            cols = slice(P * h, P * (h + 1))
+            nc.tensor.matmul_mx(y_ps[h][:], lhsT=wb_w[:, cols].bitcast(E4M3), lhsT_scale=wb_rows[:, cols],
+                                rhs=hid_w[:].bitcast(E5M2), rhs_scale=hid_s[:], start=False, stop=True)
+        nc.vector.tensor_copy(y_sb[0][:], y_ps[0][:])
+        nc.sync.dma_start(out[0:P, :], y_sb[0][:])
+        nc.scalar.copy(y_sb[1][:], y_ps[1][:])
+        nc.scalar.dma_start(out[P : 2 * P, :], y_sb[1][:])

@@ -21,7 +21,7 @@ P = 128
 PACK = 4
 QUADS = 4
 QUAD = 32
-WARM = False
+WARM = True
 ABS_SPLIT = 64
 
 

@@ -36,8 +36,8 @@ def tile_list_gatedcross_twotab_further_plain_kernel(
         sb_pool = ctx.enter_context(tc.tile_pool(name="sbuf", bufs=1))
         psum = ctx.enter_context(tc.psum_pool(name="psum", bufs=1))
 
-        def new(name, shape, dtype):
-            return sb_pool.tile(shape, dtype, name=name, align_bytes=64)
+        def new(name, shape, dtype, tag=None):
+            return sb_pool.tile(shape, dtype, name=name, tag=tag or name, align_bytes=64)
 
         def load_list(name, src):
             tile = lists.tile(list(src.shape), U16, name=name)
@@ -68,9 +68,10 @@ def tile_list_gatedcross_twotab_further_plain_kernel(
             queue.dma_start(stage[:], words.rearrange("(q r) n -> r q n", r=4))
             return stage
 
-        def spread(rows, stage):
+        def spread(pairs):
             for q in range(QUADS):
-                nc.vector.tensor_copy(rows[QUAD * q : QUAD * q + 4, :].bitcast(I32), stage[:, q, :])
+                for rows, stage in pairs:
+                    nc.vector.tensor_copy(rows[QUAD * q : QUAD * q + 4, :].bitcast(I32), stage[:, q, :])
 
         def load_vector(name, src, queue):
             tile = new(name, [P, PACK], F32)
@@ -87,41 +88,40 @@ def tile_list_gatedcross_twotab_further_plain_kernel(
             nc.vector.tensor_copy(dealt[:].rearrange("p (t m) -> p t m", t=PACK), rows[:].rearrange("p (m t) -> p t m", t=PACK))
             return dealt
 
-        def gather(name, window, offsets, dtype):
-            picked = new(name, [P, 16 * offsets.shape[1]], dtype)
+        def gather(name, window, offsets, dtype, tag=None):
+            picked = new(name, [P, 16 * offsets.shape[1]], dtype, tag)
             nc.vector.tensor_copy(picked[:], window[:].indirect(offsets[:]))
             return picked
 
-        xt_rows = zeroed_rows("xt_rows", T)
+        xo_rows = zeroed_rows("xo_rows", Z)
         if WARM:
             warm = new("warm", [P, 2], F32)
             nc.vector.memset(warm[:, 0:1], 0.0)
+        xt_rows = zeroed_rows("xt_rows", T)
         w_rows = zeroed_rows("w_rows", R)
-        xo_rows = zeroed_rows("xo_rows", Z)
         w2_rows = zeroed_rows("w2_rows", R)
         ws_rows = new("ws_rows", [P, N], U8)
         wb_rows = new("wb_rows", [P, N], U8)
 
         l1 = load_list("l1", offs)
+        xt_stage = load_scales_staged("xt_stage", xt_scales, nc.sync)
         w_stage = load_scales_staged("w_stage", w_scales, nc.sync)
         xt_w = load_words("xt_w", xt_words, U16, nc.sync)
         w_w = load_words("w_w", w_words, U32, nc.sync)
-        load_scales_direct(xt_rows, xt_scales, nc.scalar)
+        w2_stage = load_scales_staged("w2_stage", w2_scales, nc.sync)
+        l2 = load_list("l2", offs2)
+        w2_w = load_words("w2_w", w2_words, U32, nc.sync)
         if WARM:
             nc.scalar.activation(warm[:, 1:2], warm[:, 0:1], ACT.Sigmoid)
         sh_t = load_vector("sh_t", sh, nc.gpsimd)
         bh_t = load_vector("bh_t", bh, nc.gpsimd)
-        sa_t = load_vector("sa_t", sa, nc.gpsimd)
-
-        l6 = load_list("l6", offs6)
-        l2 = load_list("l2", offs2)
-        xo_stage = load_scales_staged("xo_stage", xo_scales, nc.sync)
-        w2_stage = load_scales_staged("w2_stage", w2_scales, nc.sync)
-        xo_w = load_words("xo_w", xo_words, U32, nc.sync)
-        w2_w = load_words("w2_w", w2_words, U32, nc.sync)
+        sb_t = load_vector("sb_t", sb, nc.gpsimd)
         l3 = load_list("l3", offs3)
+        sa_t = load_vector("sa_t", sa, nc.sync)
+        load_scales_direct(xo_rows, xo_scales, nc.sync)
+        xo_w = load_words("xo_w", xo_words, U32, nc.sync)
+        l6 = load_list("l6", offs6)
         l5 = load_list("l5", offs5)
-        sb_t = load_vector("sb_t", sb, nc.sync)
         l4 = load_list("l4", offs4)
         sg_t = load_vector("sg_t", sg, nc.sync)
         bg_t = load_vector("bg_t", bg, nc.sync)
@@ -131,11 +131,12 @@ def tile_list_gatedcross_twotab_further_plain_kernel(
         wb_w = load_words("wb_w", wb_words, U32, nc.sync)
         load_scales_direct(wb_rows, wb_scales, nc.sync)
 
-        spread(w_rows, w_stage)
+        spread([(xt_rows, xt_stage), (w_rows, w_stage)])
         xt_gs = gather("xt_gs", xt_rows, l1, U8)
         w_ds = deal_bytes("w_ds", w_rows)
         xt_g = gather("xt_g", xt_w, l1, U16)
         w_d = deal_words("w_d", w_w, nc.scalar.copy)
+        w2_d = deal_words("w2_d", w2_w, nc.scalar.copy)
 
         def product(tag, t, wd, wds, wfmt, xg, xgs, xfmt):
             acc = psum.tile([P, J], F32, name=tag + str(t))
@@ -151,41 +152,45 @@ def tile_list_gatedcross_twotab_further_plain_kernel(
         p2 = new("p2", [P, PACK, O], F32)
         g1 = new("g1", [P, PACK, O], F32)
 
-        def look_a(t):
-            nc.scalar.activation(g2[:, t, :], a_sb[t][:].indirect(l6[:]), ACT.Sigmoid, bias=bh_t[:, t : t + 1], scale=sh_t[:, t : t + 1])
+        def pick_a(t):
             nc.scalar.activation(p1[:, t, :], a_sb[t][:].indirect(l3[:]), ACT.Copy, scale=sa_t[:, t : t + 1])
 
-        nc.vector.tensor_copy(a_sb[0][:], a_ps[0][:])
-        look_a(0)
-        nc.scalar.copy(a_sb[1][:], a_ps[1][:])
-        look_a(1)
-        nc.scalar.copy(a_sb[2][:], a_ps[2][:])
-        look_a(2)
-        nc.scalar.copy(a_sb[3][:], a_ps[3][:])
-        look_a(3)
+        def gate_a(t):
+            nc.scalar.activation(g2[:, t, :], a_sb[t][:].indirect(l6[:]), ACT.Sigmoid, bias=bh_t[:, t : t + 1], scale=sh_t[:, t : t + 1])
 
-        spread(w2_rows, w2_stage)
-        spread(xo_rows, xo_stage)
-        w2_ds = deal_bytes("w2_ds", w2_rows)
+        nc.vector.tensor_copy(a_sb[0][:], a_ps[0][:])
+        nc.scalar.copy(a_sb[1][:], a_ps[1][:])
+        pick_a(0)
+        nc.scalar.copy(a_sb[2][:], a_ps[2][:])
+        pick_a(1)
+        pick_a(2)
+        for t in range(PACK - 1):
+            gate_a(t)
+
+        spread([(w2_rows, w2_stage)])
         xo_gs = gather("xo_gs", xo_rows, l2, U8)
+        w2_ds = deal_bytes("w2_ds", w2_rows)
         xo_g = gather("xo_g", xo_w, l2, U32)
-        w2_d = deal_words("w2_d", w2_w, nc.vector.tensor_copy)
         b_ps = [product("bank_b", t, w2_d, w2_ds, E4M3, xo_g, xo_gs, E5M2) for t in range(PACK)]
         b_sb = [new("b_sb" + str(t), [P, J], F32) for t in range(PACK)]
-
-        x7_gs = gather("x7_gs", xt_rows, l7, U8)
-        x7_g = gather("x7_g", xt_w, l7, U16)
-        y_ps = [psum.tile([P, O], F32, name="bank_a" + str(h)) for h in range(N // P)]
-        for h in range(N // P):
-            cols = slice(P * h, P * (h + 1))
-            nc.tensor.matmul_mx(y_ps[h][:], lhsT=ws_w[:, cols].bitcast(E4M3), lhsT_scale=ws_rows[:, cols],
-                                rhs=x7_g[:].bitcast(E2M1), rhs_scale=x7_gs[:], start=True, stop=False)
+        nc.vector.tensor_copy(a_sb[3][:], a_ps[3][:])
+        pick_a(3)
+        gate_a(3)
 
         u1 = new("u1", [P, PACK, O], F32)
         u2 = new("u2", [P, PACK, O], F32)
         diff = new("diff", [P, PACK, O], F32)
         for t in range(PACK):
             nc.vector.tensor_copy(b_sb[t][:], b_ps[t][:])
+
+        x7_gs = gather("x7_gs", xt_rows, l7, U8, "xo_gs")
+        x7_g = gather("x7_g", xt_w, l7, U16, "xo_g")
+        y_ps = [psum.tile([P, O], F32, name="bank_a" + str(h)) for h in range(N // P)]
+        for h in range(N // P):
+            cols = slice(P * h, P * (h + 1))
+            nc.tensor.matmul_mx(y_ps[h][:], lhsT=ws_w[:, cols].bitcast(E4M3), lhsT_scale=ws_rows[:, cols],
+                                rhs=x7_g[:].bitcast(E2M1), rhs_scale=x7_gs[:], start=True, stop=False)
+
         for t in range(PACK):
             nc.scalar.activation(p2[:, t, :], b_sb[t][:].indirect(l5[:]), ACT.Copy, scale=sb_t[:, t : t + 1])
             nc.scalar.activation(g1[:, t, :], b_sb[t][:].indirect(l4[:]), ACT.Sigmoid, bias=bg_t[:, t : t + 1], scale=sg_t[:, t : t + 1])

@@ -19,10 +19,11 @@ ALU = mybir.AluOpType
 
 P = 128
 PACK = 4
-QUADS = 4
-QUAD = 32
-WARM = True
-ABS_SPLIT = 64
+QUADRANTS = 4
+QUADRANT = P // QUADRANTS
+BLOCKS = 4
+GROUP = 16
+SCALAR_PLACES = 72
 
 
 def tile_list_gatedcross_twotab_further_plain_kernel(
@@ -33,184 +34,168 @@ def tile_list_gatedcross_twotab_further_plain_kernel(
     nc = tc.nc
     with ExitStack() as ctx:
         lists = ctx.enter_context(tc.tile_pool(name="lists", bufs=1))
-        sb_pool = ctx.enter_context(tc.tile_pool(name="sbuf", bufs=1))
+        sbuf = ctx.enter_context(tc.tile_pool(name="sbuf", bufs=1))
         psum = ctx.enter_context(tc.psum_pool(name="psum", bufs=1))
 
-        def new(name, shape, dtype, tag=None):
-            return sb_pool.tile(shape, dtype, name=name, tag=tag or name, align_bytes=64)
+        def new(name, shape, dtype, buffer=None):
+            return sbuf.tile(shape, dtype, name=name, tag=buffer or name, align_bytes=64)
 
         def load_list(name, src):
             tile = lists.tile(list(src.shape), U16, name=name)
             nc.sync.dma_start(tile[:], src)
             return tile
 
-        def load_words(name, src, dtype, queue):
-            flat = src[0] if len(src.shape) == 3 else src[0].rearrange("p n t -> p (n t)")
-            words = flat.bitcast(I32)
-            width = words.shape[1] * (2 if dtype == U16 else 1)
-            tile = new(name, [P, width], dtype)
-            queue.dma_start(tile[:].bitcast(I32), words)
+        def load_words(name, src_bytes, columns, dtype):
+            tile = new(name, [P, columns], dtype)
+            nc.sync.dma_start(tile[:].bitcast(I32), src_bytes.bitcast(I32))
             return tile
 
-        def zeroed_rows(name, width):
-            tile = new(name, [P, width], U8)
+        def load_fp8_words(name, src):
+            return load_words(name, src[0].rearrange("p n t -> p (n t)"), src.shape[2], U32)
+
+        def zeroed_rows(name, columns):
+            tile = new(name, [P, columns], U8)
             nc.vector.memset(tile[:].bitcast(I32), 0)
             return tile
 
-        def load_scales_direct(rows, src, queue):
+        def load_scale_rows(rows, src):
             words = src[0].bitcast(I32)
-            for q in range(QUADS):
-                queue.dma_start(rows[QUAD * q : QUAD * q + 4, :].bitcast(I32), words[4 * q : 4 * q + 4, :])
+            for q in range(QUADRANTS):
+                nc.sync.dma_start(
+                    rows[QUADRANT * q : QUADRANT * q + BLOCKS, :].bitcast(I32), words[BLOCKS * q : BLOCKS * (q + 1), :]
+                )
 
-        def load_scales_staged(name, src, queue):
-            words = src[0].bitcast(I32)
-            stage = new(name, [4, QUADS, words.shape[1]], I32)
-            queue.dma_start(stage[:], words.rearrange("(q r) n -> r q n", r=4))
-            return stage
-
-        def spread(pairs):
-            for q in range(QUADS):
-                for rows, stage in pairs:
-                    nc.vector.tensor_copy(rows[QUAD * q : QUAD * q + 4, :].bitcast(I32), stage[:, q, :])
-
-        def load_vector(name, src, queue):
+        def load_factors(name, src, queue):
             tile = new(name, [P, PACK], F32)
             queue.dma_start(tile[:], src.rearrange("(p t) one -> p (t one)", t=PACK))
             return tile
 
-        def deal_words(name, words, engine_copy):
-            dealt = new(name, [P, R], U32)
-            engine_copy(dealt[:].rearrange("p (t m) -> p m t", t=PACK), words[:].rearrange("p (m t) -> p m t", t=PACK))
+        def deal_words(name, words, copy):
+            dealt = new(name, [P, R], U32, "dealt_words")
+            copy(dealt[:].rearrange("p (t m) -> p m t", t=PACK), words[:].rearrange("p (m t) -> p m t", t=PACK))
             return dealt
 
-        def deal_bytes(name, rows):
-            dealt = new(name, [P, R], U8)
-            nc.vector.tensor_copy(dealt[:].rearrange("p (t m) -> p t m", t=PACK), rows[:].rearrange("p (m t) -> p t m", t=PACK))
+        def deal_scales(name, rows):
+            dealt = new(name, [P, R], U8, "dealt_scales")
+            nc.vector.tensor_copy(
+                dealt[:].rearrange("p (t m) -> p t m", t=PACK), rows[:].rearrange("p (m t) -> p t m", t=PACK)
+            )
             return dealt
 
-        def gather(name, window, offsets, dtype, tag=None):
-            picked = new(name, [P, 16 * offsets.shape[1]], dtype, tag)
+        def gather(name, window, offsets, dtype, buffer):
+            picked = new(name, [P, GROUP * offsets.shape[1]], dtype, buffer)
             nc.vector.tensor_copy(picked[:], window[:].indirect(offsets[:]))
             return picked
 
-        xo_rows = zeroed_rows("xo_rows", Z)
-        if WARM:
-            warm = new("warm", [P, 2], F32)
-            nc.vector.memset(warm[:, 0:1], 0.0)
+        def mx_pass(acc, part, words, scales, fmt, moving, moving_scales, moving_fmt, start, stop):
+            cols = slice(P * part, P * (part + 1))
+            nc.tensor.matmul_mx(
+                acc[:], lhsT=words[:, cols].bitcast(fmt), lhsT_scale=scales[:, cols],
+                rhs=moving[:].bitcast(moving_fmt), rhs_scale=moving_scales[:], start=start, stop=stop,
+            )
+
+        def fetch_scaled(dst, rows, offsets, scale, t):
+            nc.scalar.activation(dst[:, t, :], rows[t][:].indirect(offsets[:]), ACT.Copy, scale=scale[:, t : t + 1])
+
+        def fetch_gate(dst, rows, offsets, slope, offset, t):
+            nc.scalar.activation(
+                dst[:, t, :], rows[t][:].indirect(offsets[:]), ACT.Sigmoid,
+                bias=offset[:, t : t + 1], scale=slope[:, t : t + 1],
+            )
+
         xt_rows = zeroed_rows("xt_rows", T)
         w_rows = zeroed_rows("w_rows", R)
+        xo_rows = zeroed_rows("xo_rows", Z)
         w2_rows = zeroed_rows("w2_rows", R)
         ws_rows = new("ws_rows", [P, N], U8)
         wb_rows = new("wb_rows", [P, N], U8)
 
-        l1 = load_list("l1", offs)
-        xt_stage = load_scales_staged("xt_stage", xt_scales, nc.sync)
-        w_stage = load_scales_staged("w_stage", w_scales, nc.sync)
-        xt_w = load_words("xt_w", xt_words, U16, nc.sync)
-        w_w = load_words("w_w", w_words, U32, nc.sync)
-        w2_stage = load_scales_staged("w2_stage", w2_scales, nc.sync)
-        l2 = load_list("l2", offs2)
-        w2_w = load_words("w2_w", w2_words, U32, nc.sync)
-        if WARM:
-            nc.scalar.activation(warm[:, 1:2], warm[:, 0:1], ACT.Sigmoid)
-        sh_t = load_vector("sh_t", sh, nc.gpsimd)
-        bh_t = load_vector("bh_t", bh, nc.gpsimd)
-        sb_t = load_vector("sb_t", sb, nc.gpsimd)
-        l3 = load_list("l3", offs3)
-        sa_t = load_vector("sa_t", sa, nc.sync)
-        load_scales_direct(xo_rows, xo_scales, nc.sync)
-        xo_w = load_words("xo_w", xo_words, U32, nc.sync)
-        l6 = load_list("l6", offs6)
-        l5 = load_list("l5", offs5)
-        l4 = load_list("l4", offs4)
-        sg_t = load_vector("sg_t", sg, nc.sync)
-        bg_t = load_vector("bg_t", bg, nc.sync)
-        l7 = load_list("l7", offs7)
-        ws_w = load_words("ws_w", ws_words, U32, nc.sync)
-        load_scales_direct(ws_rows, ws_scales, nc.sync)
-        wb_w = load_words("wb_w", wb_words, U32, nc.sync)
-        load_scales_direct(wb_rows, wb_scales, nc.sync)
+        idx = load_list("idx", offs)
+        load_scale_rows(xt_rows, xt_scales)
+        xt_w = load_words("xt_w", xt_words[0], T, U16)
+        w_w = load_fp8_words("w_w", w_words)
+        load_scale_rows(w_rows, w_scales)
+        sa_t = load_factors("sa_t", sa, nc.gpsimd)
+        sh_t = load_factors("sh_t", sh, nc.gpsimd)
+        bh_t = load_factors("bh_t", bh, nc.gpsimd)
+        idx3 = load_list("idx3", offs3)
+        idx6 = load_list("idx6", offs6)
+        idx2 = load_list("idx2", offs2)
+        xo_w = load_fp8_words("xo_w", xo_words)
+        load_scale_rows(xo_rows, xo_scales)
+        w2_w = load_fp8_words("w2_w", w2_words)
+        load_scale_rows(w2_rows, w2_scales)
+        idx7 = load_list("idx7", offs7)
+        idx5 = load_list("idx5", offs5)
+        sb_t = load_factors("sb_t", sb, nc.sync)
+        idx4 = load_list("idx4", offs4)
+        sg_t = load_factors("sg_t", sg, nc.sync)
+        bg_t = load_factors("bg_t", bg, nc.sync)
+        ws_w = load_fp8_words("ws_w", ws_words)
+        load_scale_rows(ws_rows, ws_scales)
+        wb_w = load_fp8_words("wb_w", wb_words)
+        load_scale_rows(wb_rows, wb_scales)
 
-        spread([(xt_rows, xt_stage), (w_rows, w_stage)])
-        xt_gs = gather("xt_gs", xt_rows, l1, U8)
-        w_ds = deal_bytes("w_ds", w_rows)
-        xt_g = gather("xt_g", xt_w, l1, U16)
+        xt_gs = gather("xt_gs", xt_rows, idx, U8, "picked_scales")
+        xt_g = gather("xt_g", xt_w, idx, U16, "picked_words")
+        w_ds = deal_scales("w_ds", w_rows)
         w_d = deal_words("w_d", w_w, nc.scalar.copy)
-        w2_d = deal_words("w2_d", w2_w, nc.scalar.copy)
-
-        def product(tag, t, wd, wds, wfmt, xg, xgs, xfmt):
-            acc = psum.tile([P, J], F32, name=tag + str(t))
-            cols = slice(P * t, P * (t + 1))
-            nc.tensor.matmul_mx(acc[:], lhsT=wd[:, cols].bitcast(wfmt), lhsT_scale=wds[:, cols],
-                                rhs=xg[:].bitcast(xfmt), rhs_scale=xgs[:], start=True, stop=True)
-            return acc
-
-        a_ps = [product("bank_a", t, w_d, w_ds, E5M2, xt_g, xt_gs, E2M1) for t in range(PACK)]
+        a_ps = [psum.tile([P, J], F32, name="bank_a" + str(t)) for t in range(PACK)]
+        for t in range(PACK):
+            mx_pass(a_ps[t], t, w_d, w_ds, E5M2, xt_g, xt_gs, E2M1, True, True)
         a_sb = [new("a_sb" + str(t), [P, J], F32) for t in range(PACK)]
-        p1 = new("p1", [P, PACK, O], F32)
-        g2 = new("g2", [P, PACK, O], F32)
-        p2 = new("p2", [P, PACK, O], F32)
-        g1 = new("g1", [P, PACK, O], F32)
+        scaled_a = new("scaled_a", [P, PACK, O], F32)
+        gate_a = new("gate_a", [P, PACK, O], F32)
+        for t in range(PACK):
+            nc.vector.tensor_copy(a_sb[t][:], a_ps[t][:])
+        for t in range(PACK):
+            fetch_scaled(scaled_a, a_sb, idx3, sa_t, t)
+        for t in range(PACK):
+            fetch_gate(gate_a, a_sb, idx6, sh_t, bh_t, t)
 
-        def pick_a(t):
-            nc.scalar.activation(p1[:, t, :], a_sb[t][:].indirect(l3[:]), ACT.Copy, scale=sa_t[:, t : t + 1])
-
-        def gate_a(t):
-            nc.scalar.activation(g2[:, t, :], a_sb[t][:].indirect(l6[:]), ACT.Sigmoid, bias=bh_t[:, t : t + 1], scale=sh_t[:, t : t + 1])
-
-        nc.vector.tensor_copy(a_sb[0][:], a_ps[0][:])
-        nc.scalar.copy(a_sb[1][:], a_ps[1][:])
-        pick_a(0)
-        nc.scalar.copy(a_sb[2][:], a_ps[2][:])
-        pick_a(1)
-        pick_a(2)
-        for t in range(PACK - 1):
-            gate_a(t)
-
-        spread([(w2_rows, w2_stage)])
-        xo_gs = gather("xo_gs", xo_rows, l2, U8)
-        w2_ds = deal_bytes("w2_ds", w2_rows)
-        xo_g = gather("xo_g", xo_w, l2, U32)
-        b_ps = [product("bank_b", t, w2_d, w2_ds, E4M3, xo_g, xo_gs, E5M2) for t in range(PACK)]
+        xo_g = gather("xo_g", xo_w, idx2, U32, "picked_words")
+        xo_gs = gather("xo_gs", xo_rows, idx2, U8, "picked_scales")
+        w2_d = deal_words("w2_d", w2_w, nc.vector.tensor_copy)
+        w2_ds = deal_scales("w2_ds", w2_rows)
+        b_ps = [psum.tile([P, J], F32, name="bank_b" + str(t)) for t in range(PACK)]
+        for t in range(PACK):
+            mx_pass(b_ps[t], t, w2_d, w2_ds, E4M3, xo_g, xo_gs, E5M2, True, True)
         b_sb = [new("b_sb" + str(t), [P, J], F32) for t in range(PACK)]
-        nc.vector.tensor_copy(a_sb[3][:], a_ps[3][:])
-        pick_a(3)
-        gate_a(3)
+        for t in range(PACK):
+            nc.vector.tensor_copy(b_sb[t][:], b_ps[t][:])
 
+        x7_gs = gather("x7_gs", xt_rows, idx7, U8, "w2_rows")
+        x7_g = gather("x7_g", xt_w, idx7, U16, "w2_w")
+        y_ps = [psum.tile([P, O], F32, name="bank_a" + str(h)) for h in range(N // P)]
+        for h in range(N // P):
+            mx_pass(y_ps[h], h, ws_w, ws_rows, E4M3, x7_g, x7_gs, E2M1, True, False)
+
+        scaled_b = new("scaled_b", [P, PACK, O], F32)
+        gate_b = new("gate_b", [P, PACK, O], F32)
         u1 = new("u1", [P, PACK, O], F32)
         u2 = new("u2", [P, PACK, O], F32)
         diff = new("diff", [P, PACK, O], F32)
         for t in range(PACK):
-            nc.vector.tensor_copy(b_sb[t][:], b_ps[t][:])
-
-        x7_gs = gather("x7_gs", xt_rows, l7, U8, "xo_gs")
-        x7_g = gather("x7_g", xt_w, l7, U16, "xo_g")
-        y_ps = [psum.tile([P, O], F32, name="bank_a" + str(h)) for h in range(N // P)]
-        for h in range(N // P):
-            cols = slice(P * h, P * (h + 1))
-            nc.tensor.matmul_mx(y_ps[h][:], lhsT=ws_w[:, cols].bitcast(E4M3), lhsT_scale=ws_rows[:, cols],
-                                rhs=x7_g[:].bitcast(E2M1), rhs_scale=x7_gs[:], start=True, stop=False)
-
-        for t in range(PACK):
-            nc.scalar.activation(p2[:, t, :], b_sb[t][:].indirect(l5[:]), ACT.Copy, scale=sb_t[:, t : t + 1])
-            nc.scalar.activation(g1[:, t, :], b_sb[t][:].indirect(l4[:]), ACT.Sigmoid, bias=bg_t[:, t : t + 1], scale=sg_t[:, t : t + 1])
-            nc.vector.tensor_tensor(u2[:, t, :], p2[:, t, :], g2[:, t, :], ALU.mult)
-            nc.vector.tensor_tensor(u1[:, t, :], p1[:, t, :], g1[:, t, :], ALU.mult)
+            fetch_scaled(scaled_b, b_sb, idx5, sb_t, t)
+            fetch_gate(gate_b, b_sb, idx4, sg_t, bg_t, t)
+            nc.vector.tensor_tensor(u2[:, t, :], scaled_b[:, t, :], gate_a[:, t, :], ALU.mult)
+            nc.vector.tensor_tensor(u1[:, t, :], scaled_a[:, t, :], gate_b[:, t, :], ALU.mult)
             nc.vector.tensor_tensor(diff[:, t, :], u1[:, t, :], u2[:, t, :], ALU.subtract)
 
         hid = new("hid", [P, O, PACK], BF16)
-        woven = diff[:].rearrange("p t o -> p o t")
-        nc.scalar.activation(hid[:, :ABS_SPLIT, :], woven[:, :ABS_SPLIT, :], ACT.Abs)
-        nc.vector.scalar_tensor_tensor(hid[:, ABS_SPLIT:, :], woven[:, ABS_SPLIT:, :], -1.0, woven[:, ABS_SPLIT:, :], ALU.mult, ALU.max)
+        by_place = diff[:].rearrange("p t o -> p o t")
+        nc.scalar.activation(hid[:, :SCALAR_PLACES, :], by_place[:, :SCALAR_PLACES, :], ACT.Abs)
+        rest = by_place[:, SCALAR_PLACES:, :]
+        nc.vector.scalar_tensor_tensor(hid[:, SCALAR_PLACES:, :], rest, -1.0, rest, ALU.mult, ALU.max)
         hid_w = new("hid_w", [P, O], U32)
-        hid_s = new("hid_s", [P, O], U8)
-        nc.vector.quantize_mx(out=hid_w[:].bitcast(E5M2), scales=hid_s[:], in_=hid[:].rearrange("p o t -> p (o t)"))
+        hid_rows = new("hid_rows", [P, O], U8)
+        nc.vector.quantize_mx(
+            out=hid_w[:].bitcast(E5M2), scales=hid_rows[:], in_=hid[:].rearrange("p o t -> p (o t)")
+        )
 
         y_sb = [new("y_sb" + str(h), [P, O], F32) for h in range(N // P)]
         for h in range(N // P):
-            cols = slice(P * h, P * (h + 1))
-            nc.tensor.matmul_mx(y_ps[h][:], lhsT=wb_w[:, cols].bitcast(E4M3), lhsT_scale=wb_rows[:, cols],
-                                rhs=hid_w[:].bitcast(E5M2), rhs_scale=hid_s[:], start=False, stop=True)
+            mx_pass(y_ps[h], h, wb_w, wb_rows, E4M3, hid_w, hid_rows, E5M2, False, True)
         nc.vector.tensor_copy(y_sb[0][:], y_ps[0][:])
         nc.sync.dma_start(out[0:P, :], y_sb[0][:])
         nc.scalar.copy(y_sb[1][:], y_ps[1][:])

from contextlib import ExitStack

import concourse.mybir as mybir

K, T, J, R, F, Z, O, N = 512, 1024, 256, 512, 512, 1024, 128, 256
FLOPS = 2 * K * R * J + 2 * F * R * J + 2 * R * N * O + 2 * K * N * O

F32 = mybir.dt.float32
BF16 = mybir.dt.bfloat16
I32 = mybir.dt.int32
U32 = mybir.dt.uint32
U16 = mybir.dt.uint16
U8 = mybir.dt.uint8
E4M3 = mybir.dt.float8_e4m3fn_x4
E5M2 = mybir.dt.float8_e5m2_x4
E2M1 = mybir.dt.float4_e2m1fn_x4
ACT = mybir.ActivationFunctionType
ALU = mybir.AluOpType

P = 128
PACK = 4
QUADRANTS = 4
QUADRANT = P // QUADRANTS
BLOCKS = 4
GROUP = 16
SCALAR_PLACES = 72


def tile_list_gatedcross_twotab_further_plain_kernel(
    tc, xt_words, xt_scales, xo_words, xo_scales, w_words, w_scales, w2_words, w2_scales,
    sa, sb, sg, bg, sh, bh, wb_words, wb_scales, ws_words, ws_scales,
    offs, offs2, offs3, offs4, offs5, offs6, offs7, out,
):
    nc = tc.nc
    with ExitStack() as ctx:
        lists = ctx.enter_context(tc.tile_pool(name="lists", bufs=1))
        sbuf = ctx.enter_context(tc.tile_pool(name="sbuf", bufs=1))
        psum = ctx.enter_context(tc.psum_pool(name="psum", bufs=1))

        def new(name, shape, dtype, buffer=None):
            return sbuf.tile(shape, dtype, name=name, tag=buffer or name, align_bytes=64)

        def load_list(name, src):
            tile = lists.tile(list(src.shape), U16, name=name)
            nc.sync.dma_start(tile[:], src)
            return tile

        def load_words(name, src_bytes, columns, dtype):
            tile = new(name, [P, columns], dtype)
            nc.sync.dma_start(tile[:].bitcast(I32), src_bytes.bitcast(I32))
            return tile

        def load_fp8_words(name, src):
            return load_words(name, src[0].rearrange("p n t -> p (n t)"), src.shape[2], U32)

        def zeroed_rows(name, columns):
            tile = new(name, [P, columns], U8)
            nc.vector.memset(tile[:].bitcast(I32), 0)
            return tile

        def load_scale_rows(rows, src):
            words = src[0].bitcast(I32)
            for q in range(QUADRANTS):
                nc.sync.dma_start(
                    rows[QUADRANT * q : QUADRANT * q + BLOCKS, :].bitcast(I32), words[BLOCKS * q : BLOCKS * (q + 1), :]
                )

        def load_factors(name, src, queue):
            tile = new(name, [P, PACK], F32)
            queue.dma_start(tile[:], src.rearrange("(p t) one -> p (t one)", t=PACK))
            return tile

        def deal_words(name, words, copy):
            dealt = new(name, [P, R], U32, "dealt_words")
            copy(dealt[:].rearrange("p (t m) -> p m t", t=PACK), words[:].rearrange("p (m t) -> p m t", t=PACK))
            return dealt

        def deal_scales(name, rows):
            dealt = new(name, [P, R], U8, "dealt_scales")
            nc.vector.tensor_copy(
                dealt[:].rearrange("p (t m) -> p t m", t=PACK), rows[:].rearrange("p (m t) -> p t m", t=PACK)
            )
            return dealt

        def gather(name, window, offsets, dtype, buffer):
            picked = new(name, [P, GROUP * offsets.shape[1]], dtype, buffer)
            nc.vector.tensor_copy(picked[:], window[:].indirect(offsets[:]))
            return picked

        def mx_pass(acc, part, words, scales, fmt, moving, moving_scales, moving_fmt, start, stop):
            cols = slice(P * part, P * (part + 1))
            nc.tensor.matmul_mx(
                acc[:], lhsT=words[:, cols].bitcast(fmt), lhsT_scale=scales[:, cols],
                rhs=moving[:].bitcast(moving_fmt), rhs_scale=moving_scales[:], start=start, stop=stop,
            )

        def fetch_scaled(dst, rows, offsets, scale, t):
            nc.scalar.activation(dst[:, t, :], rows[t][:].indirect(offsets[:]), ACT.Copy, scale=scale[:, t : t + 1])

        def fetch_gate(dst, rows, offsets, slope, offset, t):
            nc.scalar.activation(
                dst[:, t, :], rows[t][:].indirect(offsets[:]), ACT.Sigmoid,
                bias=offset[:, t : t + 1], scale=slope[:, t : t + 1],
            )

        xt_rows = zeroed_rows("xt_rows", T)
        w_rows = zeroed_rows("w_rows", R)
        xo_rows = zeroed_rows("xo_rows", Z)
        w2_rows = zeroed_rows("w2_rows", R)
        ws_rows = new("ws_rows", [P, N], U8)
        wb_rows = new("wb_rows", [P, N], U8)

        idx = load_list("idx", offs)
        load_scale_rows(xt_rows, xt_scales)
        xt_w = load_words("xt_w", xt_words[0], T, U16)
        w_w = load_fp8_words("w_w", w_words)
        load_scale_rows(w_rows, w_scales)
        sa_t = load_factors("sa_t", sa, nc.gpsimd)
        sh_t = load_factors("sh_t", sh, nc.gpsimd)
        bh_t = load_factors("bh_t", bh, nc.gpsimd)
        idx3 = load_list("idx3", offs3)
        idx6 = load_list("idx6", offs6)
        idx2 = load_list("idx2", offs2)
        xo_w = load_fp8_words("xo_w", xo_words)
        load_scale_rows(xo_rows, xo_scales)
        w2_w = load_fp8_words("w2_w", w2_words)
        load_scale_rows(w2_rows, w2_scales)
        idx7 = load_list("idx7", offs7)
        idx5 = load_list("idx5", offs5)
        sb_t = load_factors("sb_t", sb, nc.sync)
        idx4 = load_list("idx4", offs4)
        sg_t = load_factors("sg_t", sg, nc.sync)
        bg_t = load_factors("bg_t", bg, nc.sync)
        ws_w = load_fp8_words("ws_w", ws_words)
        load_scale_rows(ws_rows, ws_scales)
        wb_w = load_fp8_words("wb_w", wb_words)
        load_scale_rows(wb_rows, wb_scales)

        xt_gs = gather("xt_gs", xt_rows, idx, U8, "picked_scales")
        xt_g = gather("xt_g", xt_w, idx, U16, "picked_words")
        w_ds = deal_scales("w_ds", w_rows)
        w_d = deal_words("w_d", w_w, nc.scalar.copy)
        a_ps = [psum.tile([P, J], F32, name="bank_a" + str(t)) for t in range(PACK)]
        for t in range(PACK):
            mx_pass(a_ps[t], t, w_d, w_ds, E5M2, xt_g, xt_gs, E2M1, True, True)
        a_sb = [new("a_sb" + str(t), [P, J], F32) for t in range(PACK)]
        scaled_a = new("scaled_a", [P, PACK, O], F32)
        gate_a = new("gate_a", [P, PACK, O], F32)
        for t in range(PACK):
            nc.vector.tensor_copy(a_sb[t][:], a_ps[t][:])
        for t in range(PACK):
            fetch_scaled(scaled_a, a_sb, idx3, sa_t, t)
        for t in range(PACK):
            fetch_gate(gate_a, a_sb, idx6, sh_t, bh_t, t)

        xo_g = gather("xo_g", xo_w, idx2, U32, "picked_words")
        xo_gs = gather("xo_gs", xo_rows, idx2, U8, "picked_scales")
        w2_d = deal_words("w2_d", w2_w, nc.vector.tensor_copy)
        w2_ds = deal_scales("w2_ds", w2_rows)
        b_ps = [psum.tile([P, J], F32, name="bank_b" + str(t)) for t in range(PACK)]
        for t in range(PACK):
            mx_pass(b_ps[t], t, w2_d, w2_ds, E4M3, xo_g, xo_gs, E5M2, True, True)
        b_sb = [new("b_sb" + str(t), [P, J], F32) for t in range(PACK)]
        for t in range(PACK):
            nc.vector.tensor_copy(b_sb[t][:], b_ps[t][:])

        x7_gs = gather("x7_gs", xt_rows, idx7, U8, "w2_rows")
        x7_g = gather("x7_g", xt_w, idx7, U16, "w2_w")
        y_ps = [psum.tile([P, O], F32, name="bank_a" + str(h)) for h in range(N // P)]
        for h in range(N // P):
            mx_pass(y_ps[h], h, ws_w, ws_rows, E4M3, x7_g, x7_gs, E2M1, True, False)

        scaled_b = new("scaled_b", [P, PACK, O], F32)
        gate_b = new("gate_b", [P, PACK, O], F32)
        u1 = new("u1", [P, PACK, O], F32)
        u2 = new("u2", [P, PACK, O], F32)
        diff = new("diff", [P, PACK, O], F32)
        for t in range(PACK):
            fetch_scaled(scaled_b, b_sb, idx5, sb_t, t)
            fetch_gate(gate_b, b_sb, idx4, sg_t, bg_t, t)
            nc.vector.tensor_tensor(u2[:, t, :], scaled_b[:, t, :], gate_a[:, t, :], ALU.mult)
            nc.vector.tensor_tensor(u1[:, t, :], scaled_a[:, t, :], gate_b[:, t, :], ALU.mult)
            nc.vector.tensor_tensor(diff[:, t, :], u1[:, t, :], u2[:, t, :], ALU.subtract)

        hid = new("hid", [P, O, PACK], BF16)
        by_place = diff[:].rearrange("p t o -> p o t")
        nc.scalar.activation(hid[:, :SCALAR_PLACES, :], by_place[:, :SCALAR_PLACES, :], ACT.Abs)
        rest = by_place[:, SCALAR_PLACES:, :]
        nc.vector.scalar_tensor_tensor(hid[:, SCALAR_PLACES:, :], rest, -1.0, rest, ALU.mult, ALU.max)
        hid_w = new("hid_w", [P, O], U32)
        hid_rows = new("hid_rows", [P, O], U8)
        nc.vector.quantize_mx(
            out=hid_w[:].bitcast(E5M2), scales=hid_rows[:], in_=hid[:].rearrange("p o t -> p (o t)")
        )

        y_sb = [new("y_sb" + str(h), [P, O], F32) for h in range(N // P)]
        for h in range(N // P):
            mx_pass(y_ps[h], h, wb_w, wb_rows, E4M3, hid_w, hid_rows, E5M2, False, True)
        nc.vector.tensor_copy(y_sb[0][:], y_ps[0][:])
        nc.sync.dma_start(out[0:P, :], y_sb[0][:])
        nc.scalar.copy(y_sb[1][:], y_ps[1][:])
        nc.scalar.dma_start(out[P : 2 * P, :], y_sb[1][:])
